import numpy as np
import ml_dtypes

BF16 = ml_dtypes.bfloat16


def bf(x):
    return np.asarray(x, np.float32).astype(BF16)


def f32(x):
    return np.asarray(x, np.float32)


def f64(x):
    return np.asarray(x).astype(np.float64)


def striped(idx):
    return np.tile(idx.reshape(-1, 16).T, (8, 1))


S, K, M, N, D, V = 512, 256, 256, 256, 4, 64


def setup_inputs():
    return {"table": bf(np.random.standard_normal((K, S))), "w": bf(np.random.standard_normal((D, K, M)) / np.sqrt(D * K)), "b": f32(0.5 * np.random.standard_normal((M, 1))), "offs": striped(np.random.permutation(np.tile(np.arange(S), 2))[:N])}


def reference(table, w, b, offs):
    idx = offs[:16].T.reshape(-1)
    x = f64(table)[:, idx]
    y = sum(f64(w)[t].T @ x[:, t * V : (t + 1) * V] for t in range(D))
    return np.tanh(y + f64(b))

@@ -1,0 +1,53 @@
+import concourse.mybir as mybir
+
+BF16, F32, U16 = mybir.dt.bfloat16, mybir.dt.float32, mybir.dt.uint16
+TANH = mybir.ActivationFunctionType.Tanh
+
+P = 128
+S, K, M, N = 512, 256, 256, 256
+D = 4
+V = N // D
+KB, MB = K // P, M // P
+COLS = V // 16
+
+FLOPS = 2 * D * K * M * V
+
+
+def tile_gather_matmul_kernel(tc, table, w, b, offs, out):
+    nc = tc.nc
+    with (
+        tc.tile_pool(name="held", bufs=1) as held,
+        tc.psum_pool(name="psum", bufs=1) as psum,
+    ):
+        offsets = held.tile([P, N // 16], U16, name="offsets")
+        nc.sync.dma_start(offsets[:], offs)
+
+        blocks = [held.tile([P, S], BF16, name=f"block{kb}") for kb in range(KB)]
+        for kb in range(KB):
+            nc.sync.dma_start(blocks[kb][:], table[kb * P : (kb + 1) * P, :])
+
+        weights = [held.tile([P, KB, M], BF16, name=f"weights{t}") for t in range(D)]
+        for t in range(D):
+            nc.scalar.dma_start(weights[t][:], w[t].rearrange("(kb p) m -> p kb m", p=P))
+
+        bias = held.tile([P, MB], F32, name="bias")
+        with nc.allow_non_contiguous_dma(reason="one float32 to a partition"):
+            nc.gpsimd.dma_start(bias[:], b.rearrange("(mb p) o -> p (mb o)", p=P))
+
+        sums = [psum.tile([P, V], F32, name=f"sums{mb}") for mb in range(MB)]
+        for t in range(D):
+            piece = offsets[:, t * COLS : (t + 1) * COLS]
+            for mb in range(MB):
+                for kb in range(KB):
+                    nc.tensor.matmul(
+                        sums[mb][:],
+                        weights[t][:, kb, mb * P : (mb + 1) * P],
+                        blocks[kb][:].indirect(piece),
+                        start=(t == 0 and kb == 0),
+                        stop=(t == D - 1 and kb == KB - 1),
+                    )
+
+        for mb in range(MB):
+            result = held.tile([P, V], F32, name=f"result{mb}")
+            nc.scalar.activation(result[:], sums[mb][:], TANH, bias=bias[:, mb : mb + 1])
+            nc.sync.dma_start(out[mb * P : (mb + 1) * P, :], result[:])

@@ -9,6 +9,8 @@ D = 4
 V = N // D
 KB, MB = K // P, M // P
 COLS = V // 16
+WIDTH = 256
+WARM_UP = 7
 
 FLOPS = 2 * D * K * M * V
 
@@ -22,26 +24,39 @@ def tile_gather_matmul_kernel(tc, table, w, b, offs, out):
         offsets = held.tile([P, N // 16], U16, name="offsets")
         nc.sync.dma_start(offsets[:], offs)
 
+        zeros = held.tile([P, WIDTH], BF16, name="zeros")
+        nc.vector.memset(zeros[:], 0.0)
+        idle = psum.tile([P, WIDTH], F32, name="idle")
+        for i in range(WARM_UP):
+            nc.tensor.matmul(idle[:], zeros[:, 0:P], zeros[:], start=True, stop=True)
+
         blocks = [held.tile([P, S], BF16, name=f"block{kb}") for kb in range(KB)]
-        for kb in range(KB):
-            nc.sync.dma_start(blocks[kb][:], table[kb * P : (kb + 1) * P, :])
-
-        weights = [held.tile([P, KB, M], BF16, name=f"weights{t}") for t in range(D)]
-        for t in range(D):
-            nc.scalar.dma_start(weights[t][:], w[t].rearrange("(kb p) m -> p kb m", p=P))
-
+        weights = [held.tile([P, KB * M], BF16, name=f"weights{t}") for t in range(D)]
         bias = held.tile([P, MB], F32, name="bias")
-        with nc.allow_non_contiguous_dma(reason="one float32 to a partition"):
-            nc.gpsimd.dma_start(bias[:], b.rearrange("(mb p) o -> p (mb o)", p=P))
+        table_blocks = table.rearrange("(p kb) s -> kb p s", kb=KB)
+
+        loads = [(blocks[0], table_blocks[0]), (weights[0], w[0].rearrange("(p kb) m -> p (kb m)", kb=KB))]
+        loads += [(blocks[kb], table_blocks[kb]) for kb in range(1, KB)]
+        loads += [(weights[t], w[t].rearrange("(p kb) m -> p (kb m)", kb=KB)) for t in range(1, D)]
+        loads.append((bias, b.rearrange("(mb p) o -> p (mb o)", p=P)))
+
+        with nc.allow_non_contiguous_dma(reason="the bias: one float32 to a partition"):
+            for i, (tile, source) in enumerate(loads):
+                queue = nc.scalar if i % 2 == 0 else nc.sync
+                queue.dma_start(tile[:], source)
+
+        primer = held.tile([P, 2], F32, name="primer")
+        nc.vector.memset(primer[:, 0:1], 0.0)
+        nc.scalar.activation(primer[:, 1:2], primer[:, 0:1], TANH)
 
         sums = [psum.tile([P, V], F32, name=f"sums{mb}") for mb in range(MB)]
         for t in range(D):
             piece = offsets[:, t * COLS : (t + 1) * COLS]
-            for mb in range(MB):
-                for kb in range(KB):
+            for kb in range(KB):
+                for mb in range(MB):
                     nc.tensor.matmul(
                         sums[mb][:],
-                        weights[t][:, kb, mb * P : (mb + 1) * P],
+                        weights[t][:, kb * M + mb * P : kb * M + (mb + 1) * P],
                         blocks[kb][:].indirect(piece),
                         start=(t == 0 and kb == 0),
                         stop=(t == D - 1 and kb == KB - 1),
@@ -50,4 +65,5 @@ def tile_gather_matmul_kernel(tc, table, w, b, offs, out):
         for mb in range(MB):
             result = held.tile([P, V], F32, name=f"result{mb}")
             nc.scalar.activation(result[:], sums[mb][:], TANH, bias=bias[:, mb : mb + 1])
-            nc.sync.dma_start(out[mb * P : (mb + 1) * P, :], result[:])
+            queue = nc.scalar if mb == MB - 1 else nc.sync
+            queue.dma_start(out[mb * P : (mb + 1) * P, :], result[:])

@@ -9,6 +9,7 @@ D = 4
 V = N // D
 KB, MB = K // P, M // P
 COLS = V // 16
+PAIR = 2
 WIDTH = 256
 WARM_UP = 7
 
@@ -21,8 +22,28 @@ def tile_gather_matmul_kernel(tc, table, w, b, offs, out):
         tc.tile_pool(name="held", bufs=1) as held,
         tc.psum_pool(name="psum", bufs=1) as psum,
     ):
+        blocks = [held.tile([P, S], BF16, name=f"block{kb}") for kb in range(KB)]
+        weights = [
+            [held.tile([P, PAIR, M], BF16, name=f"weights{kb}_{h}") for h in range(D // PAIR)] for kb in range(KB)
+        ]
         offsets = held.tile([P, N // 16], U16, name="offsets")
+        bias = held.tile([P, MB], F32, name="bias")
+
+        def load_block(queue, kb):
+            queue.dma_start(blocks[kb][:], table[kb * P : (kb + 1) * P, :])
+
+        def load_weights(queue, kb, h):
+            source = w[h * PAIR : (h + 1) * PAIR, kb * P : (kb + 1) * P, :]
+            queue.dma_start(weights[kb][h][:], source.rearrange("t k m -> k t m"))
+
+        load_block(nc.scalar, 0)
+        load_weights(nc.sync, 0, 0)
         nc.sync.dma_start(offsets[:], offs)
+        nc.scalar.dma_start(bias[:], b.rearrange("(mb p) o -> p (mb o)", p=P))
+        load_weights(nc.sync, 0, 1)
+        load_block(nc.sync, 1)
+        load_weights(nc.sync, 1, 0)
+        load_weights(nc.sync, 1, 1)
 
         zeros = held.tile([P, WIDTH], BF16, name="zeros")
         nc.vector.memset(zeros[:], 0.0)
@@ -30,37 +51,23 @@ def tile_gather_matmul_kernel(tc, table, w, b, offs, out):
         for i in range(WARM_UP):
             nc.tensor.matmul(idle[:], zeros[:, 0:P], zeros[:], start=True, stop=True)
 
-        blocks = [held.tile([P, S], BF16, name=f"block{kb}") for kb in range(KB)]
-        weights = [held.tile([P, KB * M], BF16, name=f"weights{t}") for t in range(D)]
-        bias = held.tile([P, MB], F32, name="bias")
-        table_blocks = table.rearrange("(p kb) s -> kb p s", kb=KB)
-
-        loads = [(blocks[0], table_blocks[0]), (weights[0], w[0].rearrange("(p kb) m -> p (kb m)", kb=KB))]
-        loads += [(blocks[kb], table_blocks[kb]) for kb in range(1, KB)]
-        loads += [(weights[t], w[t].rearrange("(p kb) m -> p (kb m)", kb=KB)) for t in range(1, D)]
-        loads.append((bias, b.rearrange("(mb p) o -> p (mb o)", p=P)))
-
-        with nc.allow_non_contiguous_dma(reason="the bias: one float32 to a partition"):
-            for i, (tile, source) in enumerate(loads):
-                queue = nc.scalar if i % 2 == 0 else nc.sync
-                queue.dma_start(tile[:], source)
-
         primer = held.tile([P, 2], F32, name="primer")
         nc.vector.memset(primer[:, 0:1], 0.0)
         nc.scalar.activation(primer[:, 1:2], primer[:, 0:1], TANH)
 
         sums = [psum.tile([P, V], F32, name=f"sums{mb}") for mb in range(MB)]
-        for t in range(D):
-            piece = offsets[:, t * COLS : (t + 1) * COLS]
-            for kb in range(KB):
+        for kb in range(KB):
+            for h in range(D // PAIR):
                 for mb in range(MB):
-                    nc.tensor.matmul(
-                        sums[mb][:],
-                        weights[t][:, kb * M + mb * P : kb * M + (mb + 1) * P],
-                        blocks[kb][:].indirect(piece),
-                        start=(t == 0 and kb == 0),
-                        stop=(t == D - 1 and kb == KB - 1),
-                    )
+                    for j in range(PAIR):
+                        t = h * PAIR + j
+                        nc.tensor.matmul(
+                            sums[mb][:],
+                            weights[kb][h][:, j, mb * P : (mb + 1) * P],
+                            blocks[kb][:].indirect(offsets[:, t * COLS : (t + 1) * COLS]),
+                            start=(kb == 0 and t == 0),
+                            stop=(kb == KB - 1 and t == D - 1),
+                        )
 
         for mb in range(MB):
             result = held.tile([P, V], F32, name=f"result{mb}")

@@ -36,14 +36,14 @@ def tile_gather_matmul_kernel(tc, table, w, b, offs, out):
             source = w[h * PAIR : (h + 1) * PAIR, kb * P : (kb + 1) * P, :]
             queue.dma_start(weights[kb][h][:], source.rearrange("t k m -> k t m"))
 
+        nc.sync.dma_start(offsets[:], offs)
         load_block(nc.scalar, 0)
         load_weights(nc.sync, 0, 0)
-        nc.sync.dma_start(offsets[:], offs)
-        nc.scalar.dma_start(bias[:], b.rearrange("(mb p) o -> p (mb o)", p=P))
-        load_weights(nc.sync, 0, 1)
+        load_weights(nc.scalar, 0, 1)
         load_block(nc.sync, 1)
-        load_weights(nc.sync, 1, 0)
+        load_weights(nc.scalar, 1, 0)
         load_weights(nc.sync, 1, 1)
+        nc.scalar.dma_start(bias[:], b.rearrange("(mb p) o -> p (mb o)", p=P))
 
         zeros = held.tile([P, WIDTH], BF16, name="zeros")
         nc.vector.memset(zeros[:], 0.0)

@@ -9,7 +9,7 @@ D = 4
 V = N // D
 KB, MB = K // P, M // P
 COLS = V // 16
-PAIR = 2
+PER_LOAD = [2, 1]
 WIDTH = 256
 WARM_UP = 7
 
@@ -22,28 +22,28 @@ def tile_gather_matmul_kernel(tc, table, w, b, offs, out):
         tc.tile_pool(name="held", bufs=1) as held,
         tc.psum_pool(name="psum", bufs=1) as psum,
     ):
-        blocks = [held.tile([P, S], BF16, name=f"block{kb}") for kb in range(KB)]
-        weights = [
-            [held.tile([P, PAIR, M], BF16, name=f"weights{kb}_{h}") for h in range(D // PAIR)] for kb in range(KB)
-        ]
         offsets = held.tile([P, N // 16], U16, name="offsets")
-        bias = held.tile([P, MB], F32, name="bias")
-
-        def load_block(queue, kb):
-            queue.dma_start(blocks[kb][:], table[kb * P : (kb + 1) * P, :])
-
-        def load_weights(queue, kb, h):
-            source = w[h * PAIR : (h + 1) * PAIR, kb * P : (kb + 1) * P, :]
-            queue.dma_start(weights[kb][h][:], source.rearrange("t k m -> k t m"))
-
         nc.sync.dma_start(offsets[:], offs)
-        load_block(nc.scalar, 0)
-        load_weights(nc.sync, 0, 0)
-        load_weights(nc.scalar, 0, 1)
-        load_block(nc.sync, 1)
-        load_weights(nc.scalar, 1, 0)
-        load_weights(nc.sync, 1, 1)
-        nc.scalar.dma_start(bias[:], b.rearrange("(mb p) o -> p (mb o)", p=P))
+
+        bias = held.tile([P, MB], F32, name="bias")
+        nc.gpsimd.dma_start(bias[:], b.rearrange("(mb p) o -> p (mb o)", p=P))
+
+        blocks = []
+        weights = []
+        loads = []
+        for kb in range(KB):
+            rows = slice(kb * P, (kb + 1) * P)
+            blocks.append(held.tile([P, S], BF16, name=f"block{kb}"))
+            loads.append((blocks[kb], table[rows, :]))
+            weights.append([])
+            for t in range(0, D, PER_LOAD[kb]):
+                piece = held.tile([P, PER_LOAD[kb], M], BF16, name=f"weights{kb}_{t}")
+                weights[kb].append(piece)
+                loads.append((piece, w[t : t + PER_LOAD[kb], rows, :].rearrange("t k m -> k t m")))
+
+        for i, (tile, source) in enumerate(loads):
+            queue = nc.scalar if i % 2 == 0 else nc.sync
+            queue.dma_start(tile[:], source)
 
         zeros = held.tile([P, WIDTH], BF16, name="zeros")
         nc.vector.memset(zeros[:], 0.0)
@@ -57,13 +57,13 @@ def tile_gather_matmul_kernel(tc, table, w, b, offs, out):
 
         sums = [psum.tile([P, V], F32, name=f"sums{mb}") for mb in range(MB)]
         for kb in range(KB):
-            for h in range(D // PAIR):
+            for h, piece in enumerate(weights[kb]):
                 for mb in range(MB):
-                    for j in range(PAIR):
-                        t = h * PAIR + j
+                    for j in range(PER_LOAD[kb]):
+                        t = h * PER_LOAD[kb] + j
                         nc.tensor.matmul(
                             sums[mb][:],
-                            weights[kb][h][:, j, mb * P : (mb + 1) * P],
+                            piece[:, j, mb * P : (mb + 1) * P],
                             blocks[kb][:].indirect(offsets[:, t * COLS : (t + 1) * COLS]),
                             start=(kb == 0 and t == 0),
                             stop=(kb == KB - 1 and t == D - 1),

@@ -10,6 +10,7 @@ V = N // D
 KB, MB = K // P, M // P
 COLS = V // 16
 PER_LOAD = [2, 1]
+SQ = 32
 WIDTH = 256
 WARM_UP = 7
 
@@ -25,8 +26,16 @@ def tile_gather_matmul_kernel(tc, table, w, b, offs, out):
         offsets = held.tile([P, N // 16], U16, name="offsets")
         nc.sync.dma_start(offsets[:], offs)
 
-        bias = held.tile([P, MB], F32, name="bias")
-        nc.gpsimd.dma_start(bias[:], b.rearrange("(mb p) o -> p (mb o)", p=P))
+        rows = held.tile([P, MB * SQ], F32, name="rows", align_bytes=64)
+        nc.gpsimd.memset(rows[:], 0.0)
+        nc.gpsimd.dma_start(
+            rows[0:P:SQ, :].rearrange("g (mb i) -> g mb i", mb=MB),
+            b.rearrange("(mb g i) o -> g mb (i o)", mb=MB, i=SQ),
+        )
+        bias = held.tile([P, MB * SQ], F32, name="bias", align_bytes=64)
+        for mb in range(MB):
+            square = slice(mb * SQ, (mb + 1) * SQ)
+            nc.vector.transpose(bias[:, square], rows[:, square])
 
         blocks = []
         weights = []
@@ -71,6 +80,6 @@ def tile_gather_matmul_kernel(tc, table, w, b, offs, out):
 
         for mb in range(MB):
             result = held.tile([P, V], F32, name=f"result{mb}")
-            nc.scalar.activation(result[:], sums[mb][:], TANH, bias=bias[:, mb : mb + 1])
+            nc.scalar.activation(result[:], sums[mb][:], TANH, bias=bias[:, mb * SQ : mb * SQ + 1])
             queue = nc.scalar if mb == MB - 1 else nc.sync
             queue.dma_start(out[mb * P : (mb + 1) * P, :], result[:])

@@ -10,6 +10,7 @@ V = N // D
 KB, MB = K // P, M // P
 COLS = V // 16
 PER_LOAD = [2, 1]
+ALIGN = 1024
 SQ = 32
 WIDTH = 256
 WARM_UP = 7
@@ -41,14 +42,14 @@ def tile_gather_matmul_kernel(tc, table, w, b, offs, out):
         weights = []
         loads = []
         for kb in range(KB):
-            rows = slice(kb * P, (kb + 1) * P)
-            blocks.append(held.tile([P, S], BF16, name=f"block{kb}"))
-            loads.append((blocks[kb], table[rows, :]))
+            rows_of_k = slice(kb * P, (kb + 1) * P)
+            blocks.append(held.tile([P, S], BF16, name=f"block{kb}", align_bytes=ALIGN))
+            loads.append((blocks[kb], table[rows_of_k, :]))
             weights.append([])
             for t in range(0, D, PER_LOAD[kb]):
-                piece = held.tile([P, PER_LOAD[kb], M], BF16, name=f"weights{kb}_{t}")
+                piece = held.tile([P, PER_LOAD[kb], M], BF16, name=f"weights{kb}_{t}", align_bytes=ALIGN)
                 weights[kb].append(piece)
-                loads.append((piece, w[t : t + PER_LOAD[kb], rows, :].rearrange("t k m -> k t m")))
+                loads.append((piece, w[t : t + PER_LOAD[kb], rows_of_k, :].rearrange("t k m -> k t m")))
 
         for i, (tile, source) in enumerate(loads):
             queue = nc.scalar if i % 2 == 0 else nc.sync
@@ -79,7 +80,7 @@ def tile_gather_matmul_kernel(tc, table, w, b, offs, out):
                         )
 
         for mb in range(MB):
-            result = held.tile([P, V], F32, name=f"result{mb}")
+            result = held.tile([P, V], F32, name=f"result{mb}", align_bytes=ALIGN)
             nc.scalar.activation(result[:], sums[mb][:], TANH, bias=bias[:, mb * SQ : mb * SQ + 1])
             queue = nc.scalar if mb == MB - 1 else nc.sync
             queue.dma_start(out[mb * P : (mb + 1) * P, :], result[:])

import concourse.mybir as mybir

BF16, F32, U16 = mybir.dt.bfloat16, mybir.dt.float32, mybir.dt.uint16
TANH = mybir.ActivationFunctionType.Tanh

P = 128
S, K, M, N = 512, 256, 256, 256
D = 4
V = N // D
KB, MB = K // P, M // P
COLS = V // 16
PER_LOAD = [2, 1]
ALIGN = 1024
SQ = 32
WIDTH = 256
WARM_UP = 7

FLOPS = 2 * D * K * M * V


def tile_gather_matmul_kernel(tc, table, w, b, offs, out):
    nc = tc.nc
    with (
        tc.tile_pool(name="held", bufs=1) as held,
        tc.psum_pool(name="psum", bufs=1) as psum,
    ):
        offsets = held.tile([P, N // 16], U16, name="offsets")
        nc.sync.dma_start(offsets[:], offs)

        rows = held.tile([P, MB * SQ], F32, name="rows", align_bytes=64)
        nc.gpsimd.memset(rows[:], 0.0)
        nc.gpsimd.dma_start(
            rows[0:P:SQ, :].rearrange("g (mb i) -> g mb i", mb=MB),
            b.rearrange("(mb g i) o -> g mb (i o)", mb=MB, i=SQ),
        )
        bias = held.tile([P, MB * SQ], F32, name="bias", align_bytes=64)
        for mb in range(MB):
            square = slice(mb * SQ, (mb + 1) * SQ)
            nc.vector.transpose(bias[:, square], rows[:, square])

        blocks = []
        weights = []
        loads = []
        for kb in range(KB):
            rows_of_k = slice(kb * P, (kb + 1) * P)
            blocks.append(held.tile([P, S], BF16, name=f"block{kb}", align_bytes=ALIGN))
            loads.append((blocks[kb], table[rows_of_k, :]))
            weights.append([])
            for t in range(0, D, PER_LOAD[kb]):
                piece = held.tile([P, PER_LOAD[kb], M], BF16, name=f"weights{kb}_{t}", align_bytes=ALIGN)
                weights[kb].append(piece)
                loads.append((piece, w[t : t + PER_LOAD[kb], rows_of_k, :].rearrange("t k m -> k t m")))

        for i, (tile, source) in enumerate(loads):
            queue = nc.scalar if i % 2 == 0 else nc.sync
            queue.dma_start(tile[:], source)

        zeros = held.tile([P, WIDTH], BF16, name="zeros")
        nc.vector.memset(zeros[:], 0.0)
        idle = psum.tile([P, WIDTH], F32, name="idle")
        for i in range(WARM_UP):
            nc.tensor.matmul(idle[:], zeros[:, 0:P], zeros[:], start=True, stop=True)

        primer = held.tile([P, 2], F32, name="primer")
        nc.vector.memset(primer[:, 0:1], 0.0)
        nc.scalar.activation(primer[:, 1:2], primer[:, 0:1], TANH)

        sums = [psum.tile([P, V], F32, name=f"sums{mb}") for mb in range(MB)]
        for kb in range(KB):
            for h, piece in enumerate(weights[kb]):
                for mb in range(MB):
                    for j in range(PER_LOAD[kb]):
                        t = h * PER_LOAD[kb] + j
                        nc.tensor.matmul(
                            sums[mb][:],
                            piece[:, j, mb * P : (mb + 1) * P],
                            blocks[kb][:].indirect(offsets[:, t * COLS : (t + 1) * COLS]),
                            start=(kb == 0 and t == 0),
                            stop=(kb == KB - 1 and t == D - 1),
                        )

        for mb in range(MB):
            result = held.tile([P, V], F32, name=f"result{mb}", align_bytes=ALIGN)
            nc.scalar.activation(result[:], sums[mb][:], TANH, bias=bias[:, mb * SQ : mb * SQ + 1])
            queue = nc.scalar if mb == MB - 1 else nc.sync
            queue.dma_start(out[mb * P : (mb + 1) * P, :], result[:])
